import numpy as np
import ml_dtypes


def mxq(x, axis, fmt="e4m3"):
    dtype, down = {"e4m3": (ml_dtypes.float8_e4m3fn, 7), "e5m2": (ml_dtypes.float8_e5m2, 14)}[fmt]
    v = np.moveaxis(np.asarray(x, np.float32).astype(ml_dtypes.bfloat16).astype(np.float64), axis, -1)
    blocks = v.reshape(v.shape[:-1] + (-1, 32))
    amax = np.abs(blocks).max(-1, keepdims=True)
    byte = np.maximum(np.where(amax > 0, np.frexp(amax)[1] - 1 + 127, 0) - down, 1)
    scale = np.exp2(byte - 127.0)
    codes = (blocks / scale).astype(np.float32).astype(dtype).astype(np.float64)
    return np.moveaxis((codes * scale).reshape(v.shape), -1, axis)


WIDE = False


def mx_kscale(k):
    if not WIDE:
        return np.ones(k)
    levels = np.array([10, -10, 5, -5, 0])
    if k % 512:
        return np.exp2(np.random.permutation(np.resize(levels, k // 32))).repeat(32)
    a = np.empty((k // 512, 16))
    for p in range(k // 512):
        a[p, :8] = np.random.permutation(np.resize(levels, 8))
        for g in range(8):
            far = levels[np.abs(levels - a[p, g]) >= 10]
            a[p, g + 8] = far[np.random.randint(len(far))]
    return np.exp2(a.ravel()).repeat(32)


def f64(x):
    return np.asarray(x).astype(np.float64)


def striped(idx):
    return np.tile(np.asarray(idx).reshape(-1, 16).T, (8, 1)).astype(np.uint16)


def unstriped(offs):
    return offs[:16].T.reshape(-1).astype(np.int64)


E2M1 = np.array([0.0, 0.5, 1.0, 1.5, 2.0, 3.0, 4.0, 6.0, -0.0, -0.5, -1.0, -1.5, -2.0, -3.0, -4.0, -6.0])


def pack_weight(w, fmt):
    k, n = w.shape
    w = f64(np.asarray(w, np.float32).astype(ml_dtypes.bfloat16)).reshape(k // 32, 32, n)
    amax = np.abs(w).max(1)
    if fmt == "e4m3":
        byte = np.frexp(amax)[1] - 1 + 127 - 7
    else:
        mant, ex = np.frexp(amax / 6.0)
        byte = np.where(mant > 0.5, ex, ex - 1) + 127
    byte = np.clip(np.where(amax > 0, byte, 1), 1, 254)
    scaled = (w * np.exp2(127.0 - byte)[:, None, :]).reshape(k, n).astype(np.float32)
    by_word = np.ascontiguousarray(scaled.reshape(k // 512, 128, 4, n).transpose(0, 1, 3, 2))
    if fmt == "e4m3":
        words = by_word.astype(ml_dtypes.float8_e4m3fn).view(np.uint8)
    else:
        c = by_word.astype(ml_dtypes.float4_e2m1fn).view(np.uint8) & 0xF
        words = (c[..., 0::2] | (c[..., 1::2] << 4)).reshape(k // 512, 128, 2 * n)
    return np.ascontiguousarray(words), np.ascontiguousarray(byte.astype(np.uint8).reshape(k // 512, 16, n))


def unpack_weight(words, scales, fmt):
    g, _, n = scales.shape
    words = np.ascontiguousarray(words).reshape(g, 128, n, -1)
    if fmt == "e4m3":
        vals = words.view(ml_dtypes.float8_e4m3fn).astype(np.float64)
    else:
        nib = np.empty((g, 128, n, 4), np.uint8)
        nib[..., 0::2] = words & 0xF
        nib[..., 1::2] = words >> 4
        vals = E2M1[nib]
    vals = vals * np.repeat(np.exp2(scales.astype(np.float64) - 127.0), 8, axis=1)[..., None]
    return vals.transpose(0, 1, 3, 2).reshape(g * 512, n)


def bf(x):
    return np.asarray(x, np.float32).astype(ml_dtypes.bfloat16)


def planes(Y):
    r, m = Y.shape
    b = f64(bf(Y)).reshape(r // 32, 32, m)
    amax = np.abs(b).max(1)
    byte = np.clip(np.where(amax > 0, np.frexp(amax)[1] - 1 + 127 - 7, 1), 1, 254)
    codes = (b * np.exp2(127.0 - byte)[:, None, :]).reshape(r, m).astype(np.float32).astype(ml_dtypes.float8_e4m3fn).view(np.uint8)
    words = codes.reshape(r // 512, 128, 4, m).transpose(0, 1, 3, 2)
    return np.ascontiguousarray(words), np.ascontiguousarray(byte.astype(np.uint8).reshape(r // 512, 16, m))


D, E, T, I, Q = 512, 512, 1024, 256, 512


def setup_inputs():
    n = np.random.standard_normal
    idx = np.random.permutation(T)[:I]
    idx2 = np.random.permutation(T)[:I]
    fd = mx_kscale(D)
    fq = mx_kscale(Q)
    keysp = pack_weight(n((D, T)) / fd[:, None], "e4m3")
    return {
        "query": (n((D, Q)) * 0.5 / np.sqrt(D) * fd[:, None]).astype(np.float32),
        "qs": (np.random.uniform(8.0, 32.0, (Q, 1)) * fq[:, None]).astype(np.float32),
        "grows": (n((Q, E)) / fq[:, None]).astype(np.float32),
        "keys_words": keysp[0],
        "keys_scales": keysp[1],
        "cross": (n((E, T))).astype(np.float32),
        "share": (np.random.uniform(0.4, 1.2, (E, 1))).astype(np.float32),
        "sg": (np.random.uniform(0.5, 2.0, (1, I))).astype(np.float32),
        "old": (0.5 * n((E, I))).astype(np.float32),
        "offs": striped(idx),
        "offs2": striped(idx2),
    }


def reference(query, qs, grows, keys_words, keys_scales, cross, share, sg, old, offs, offs2):
    idx = unstriped(offs)
    idx2 = unstriped(offs2)
    keysu = unpack_weight(keys_words, keys_scales, "e4m3")
    queryq = mxq(f64(query), 0, "e4m3")
    keysidxg = keysu[:, idx]
    a = queryq.T @ keysidxg
    p = np.exp(a - np.max(a, axis=1, keepdims=True))
    w = p * f64(qs) / np.sum(p, axis=1, keepdims=True)
    growsq = mxq(f64(grows), 0, "e4m3")
    wq = mxq(w, 0, "e4m3")
    c0 = growsq.T @ wq
    dx1 = c0 * f64(cross)[:, idx2] + c0 * f64(share)
    y = dx1 * f64(sg) + f64(old)
    words, scales = planes(y)
    return y, words, scales

@@ -1,0 +1,180 @@
+from contextlib import ExitStack
+
+import concourse.mybir as mybir
+from concourse.masks import make_identity
+
+D, E, T, I, Q = 512, 512, 1024, 256, 512
+FLOPS = 2 * D * Q * I + 2 * Q * E * I
+
+F32 = mybir.dt.float32
+BF16 = mybir.dt.bfloat16
+I32 = mybir.dt.int32
+U32 = mybir.dt.uint32
+U16 = mybir.dt.uint16
+U8 = mybir.dt.uint8
+FP8X4 = mybir.dt.float8_e4m3fn_x4
+ALU = mybir.AluOpType
+ACT = mybir.ActivationFunctionType
+AX = mybir.AxisListType
+
+P = 128
+PACK = 4
+RUN = 4
+
+
+def tile_attend_bvcrossed_d_pl_kernel(
+    tc, query, qs, grows, keys_words, keys_scales, cross, share, sg, old, offs, offs2, out_0, out_1, out_2
+):
+    nc = tc.nc
+    with ExitStack() as ctx:
+        sb = ctx.enter_context(tc.tile_pool(name="sb", bufs=1))
+        ps = ctx.enter_context(tc.psum_pool(name="ps", bufs=1))
+
+        key_list = sb.tile([P, I // 16], U16, name="key_list")
+        cross_list = sb.tile([P, I // 16], U16, name="cross_list")
+        query_raw = sb.tile([P, PACK, Q], F32, name="query_raw")
+        grows_raw = sb.tile([P, PACK, E], F32, name="grows_raw")
+        pool_words = sb.tile([P, T], I32, name="pool_words", align_bytes=64)
+        pool_scales = sb.tile([P, T], U8, name="pool_scales", align_bytes=64)
+        cross_sb = [sb.tile([P, T], F32, name="cross%d" % t) for t in range(PACK)]
+        old_sb = sb.tile([P, PACK, I], F32, name="old_sb")
+        qs_sb = sb.tile([P, PACK], F32, name="qs_sb")
+        share_sb = sb.tile([P, PACK], F32, name="share_sb")
+        sg_cols = sb.tile([P, 2], F32, name="sg_cols")
+        ident = sb.tile([P, P], F32, name="ident")
+        warm = sb.tile([P, 1], F32, name="warm")
+
+        nc.vector.memset(pool_scales[:].bitcast(I32), 0)
+        nc.vector.memset(warm[:], 0.0)
+        nc.scalar.activation(warm[:], warm[:], ACT.Exp)
+
+        nc.sync.dma_start(key_list[:], offs)
+        nc.sync.dma_start(query_raw[:], query.rearrange("(p j) q -> p j q", j=PACK))
+        for quad in range(4):
+            nc.sync.dma_start(
+                pool_scales[32 * quad : 32 * quad + 4, :].bitcast(I32),
+                keys_scales[0][4 * quad : 4 * quad + 4, :].bitcast(I32),
+            )
+        nc.sync.dma_start(pool_words[:], keys_words[0].rearrange("p n t -> p (n t)").bitcast(I32))
+        nc.sync.dma_start(grows_raw[:], grows.rearrange("(p j) e -> p j e", j=PACK))
+        nc.sync.dma_start(sg_cols[:], sg.rearrange("o (p c) -> (o p) c", c=2))
+        nc.sync.dma_start(qs_sb[:], qs.rearrange("(p r) o -> p (r o)", r=PACK))
+        cross_rows = cross.rearrange("(p t) n -> p t n", t=PACK)
+        nc.sync.dma_start(cross_sb[0][:], cross_rows[:, 0, :])
+        nc.sync.dma_start(cross_list[:], offs2)
+        nc.sync.dma_start(share_sb[:], share.rearrange("(p t) o -> p (t o)", t=PACK))
+        for t in range(1, PACK):
+            nc.sync.dma_start(cross_sb[t][:], cross_rows[:, t, :])
+        nc.sync.dma_start(old_sb[:], old.rearrange("(p t) i -> p t i", t=PACK))
+
+        make_identity(nc, ident[:])
+
+        sg_rows = ps.tile([P, 2, P], F32, name="sg_rows")
+        for c in range(2):
+            nc.tensor.transpose(sg_rows[:, c, :], sg_cols[:, c : c + 1].to_broadcast([P, P]), ident[:])
+
+        def deal(copy, raw, half, name):
+            dealt = sb.tile([P, 2, P, PACK], BF16, name=name, align_bytes=64)
+            src = raw[:].rearrange("p j (s r) -> p s j r", r=PACK)[:, :, :, 2 * half : 2 * half + 2]
+            copy(dealt[:].rearrange("p r s j -> p s j r"), src)
+            return dealt
+
+        def quantize(flat, name):
+            width = flat.shape[1] // PACK
+            codes = sb.tile([P, width], I32, name=name + "_codes", align_bytes=64)
+            scales = sb.tile([P, width], U8, name=name + "_scales", align_bytes=64)
+            nc.vector.quantize_mx(out=codes[:].bitcast(FP8X4), scales=scales[:], in_=flat)
+            return codes, scales
+
+        def weave(copy, dst, src):
+            copy(dst.rearrange("p (c i) t -> p c t i", i=RUN), src.rearrange("p t (c i) -> p c t i", i=RUN))
+
+        key_words = sb.tile([P, I], U32, name="key_words", align_bytes=64)
+        key_scales = sb.tile([P, I], U8, name="key_scales", align_bytes=64)
+
+        query_dealt = [
+            deal(nc.vector.tensor_copy, query_raw, 0, "query_dealt0"),
+            deal(nc.scalar.copy, query_raw, 1, "query_dealt1"),
+        ]
+        nc.vector.tensor_copy(key_scales[:], pool_scales[:].indirect(key_list[:]))
+        query_mx = [
+            quantize(query_dealt[h][:].rearrange("p r s j -> p (r s j)"), "query%d" % h) for h in range(2)
+        ]
+        nc.vector.tensor_copy(key_words[:], pool_words[:].bitcast(U32).indirect(key_list[:]))
+
+        neg_max = sb.tile([P, PACK], F32, name="neg_max")
+        row_sum = sb.tile([P, PACK], F32, name="row_sum")
+        inv_sum = sb.tile([P, PACK], F32, name="inv_sum")
+        probs = sb.tile([P, PACK, I], F32, name="probs")
+        w_rows = sb.tile([P, PACK, I], BF16, name="w_rows")
+        for r in range(PACK):
+            codes, scales = query_mx[r // 2]
+            cols = slice((r % 2) * P, (r % 2 + 1) * P)
+            scores = ps.tile([P, I], F32, name="scores%d" % r)
+            nc.tensor.matmul_mx(
+                out=scores[:],
+                lhsT=codes[:, cols].bitcast(FP8X4),
+                lhsT_scale=scales[:, cols],
+                rhs=key_words[:].bitcast(FP8X4),
+                rhs_scale=key_scales[:],
+                start=True,
+                stop=True,
+            )
+            nc.vector.tensor_reduce(neg_max[:, r : r + 1], scores[:], AX.X, ALU.max, negate=True)
+            nc.scalar.activation(
+                probs[:, r, :], scores[:], ACT.Exp, bias=neg_max[:, r : r + 1], accum_out=row_sum[:, r : r + 1]
+            )
+        for r in range(PACK):
+            nc.vector.reciprocal(inv_sum[:, r : r + 1], row_sum[:, r : r + 1])
+            nc.vector.tensor_scalar(
+                w_rows[:, r, :], probs[:, r, :], inv_sum[:, r : r + 1], qs_sb[:, r : r + 1], ALU.mult, ALU.mult
+            )
+        grows_dealt = [deal(nc.scalar.copy, grows_raw, h, "grows_dealt%d" % h) for h in range(2)]
+
+        w_woven = sb.tile([P, I, PACK], BF16, name="w_woven", align_bytes=64)
+        weave(nc.vector.tensor_copy, w_woven[:], w_rows[:])
+        w_codes, w_scales = quantize(w_woven[:].rearrange("p i t -> p (i t)"), "w")
+
+        y = sb.tile([P, PACK, I], F32, name="y")
+        out_rows = out_0.rearrange("(p t) i -> p t i", t=PACK)
+        for h in range(2):
+            codes, scales = quantize(grows_dealt[h][:].rearrange("p r s j -> p (r s j)"), "grows%d" % h)
+            c0 = ps.tile([P, 2, I], F32, name="c0_%d" % h)
+            for u in range(2):
+                cols = slice(u * P, (u + 1) * P)
+                nc.tensor.matmul_mx(
+                    out=c0[:, u, :],
+                    lhsT=codes[:, cols].bitcast(FP8X4),
+                    lhsT_scale=scales[:, cols],
+                    rhs=w_codes[:].bitcast(FP8X4),
+                    rhs_scale=w_scales[:],
+                    start=True,
+                    stop=True,
+                )
+            for u in range(2):
+                t = 2 * h + u
+                picked = sb.tile([P, I], F32, name="picked%d" % t)
+                factor = sb.tile([P, I], F32, name="factor%d" % t)
+                prod = sb.tile([P, I], F32, name="prod%d" % t)
+                nc.vector.tensor_copy(picked[:], cross_sb[t][:].indirect(cross_list[:]))
+                nc.vector.scalar_tensor_tensor(
+                    factor[:].rearrange("p (n c) -> p n c", c=2),
+                    picked[:].rearrange("p (n c) -> p n c", c=2),
+                    share_sb[:, t : t + 1],
+                    sg_rows[:].rearrange("p c n -> p n c"),
+                    ALU.add,
+                    ALU.mult,
+                )
+                nc.vector.tensor_tensor(prod[:], c0[:, u, :], factor[:], ALU.mult)
+                nc.vector.tensor_tensor(y[:, t, :], prod[:], old_sb[:, t, :], ALU.add)
+                nc.sync.dma_start(out_rows[:, t, :], y[:, t, :])
+
+        y_woven = sb.tile([P, I, PACK], BF16, name="y_woven", align_bytes=64)
+        weave(nc.vector.tensor_copy, y_woven[:], y[:])
+        y_codes, y_scales = quantize(y_woven[:].rearrange("p i t -> p (i t)"), "y")
+        nc.sync.dma_start(out_1[0].rearrange("p n t -> p (n t)").bitcast(I32), y_codes[:])
+        for quad in range(4):
+            nc.sync.dma_start(
+                out_2[0][4 * quad : 4 * quad + 4, :].bitcast(I32),
+                y_scales[32 * quad : 32 * quad + 4, :].bitcast(I32),
+            )

@@ -1,7 +1,6 @@
 from contextlib import ExitStack
 
 import concourse.mybir as mybir
-from concourse.masks import make_identity
 
 D, E, T, I, Q = 512, 512, 1024, 256, 512
 FLOPS = 2 * D * Q * I + 2 * Q * E * I
@@ -32,46 +31,55 @@ def tile_attend_bvcrossed_d_pl_kernel(
 
         key_list = sb.tile([P, I // 16], U16, name="key_list")
         cross_list = sb.tile([P, I // 16], U16, name="cross_list")
-        query_raw = sb.tile([P, PACK, Q], F32, name="query_raw")
-        grows_raw = sb.tile([P, PACK, E], F32, name="grows_raw")
         pool_words = sb.tile([P, T], I32, name="pool_words", align_bytes=64)
-        pool_scales = sb.tile([P, T], U8, name="pool_scales", align_bytes=64)
-        cross_sb = [sb.tile([P, T], F32, name="cross%d" % t) for t in range(PACK)]
-        old_sb = sb.tile([P, PACK, I], F32, name="old_sb")
-        qs_sb = sb.tile([P, PACK], F32, name="qs_sb")
-        share_sb = sb.tile([P, PACK], F32, name="share_sb")
-        sg_cols = sb.tile([P, 2], F32, name="sg_cols")
-        ident = sb.tile([P, P], F32, name="ident")
         warm = sb.tile([P, 1], F32, name="warm")
+        pool_scales = sb.tile([P, T], U8, name="pool_scales", align_bytes=64)
+        ident = sb.tile([P, P], F32, name="ident")
 
         nc.vector.memset(pool_scales[:].bitcast(I32), 0)
-        nc.vector.memset(warm[:], 0.0)
-        nc.scalar.activation(warm[:], warm[:], ACT.Exp)
 
         nc.sync.dma_start(key_list[:], offs)
-        nc.sync.dma_start(query_raw[:], query.rearrange("(p j) q -> p j q", j=PACK))
+        nc.sync.dma_start(pool_words[:], keys_words[0].rearrange("p n t -> p (n t)").bitcast(I32))
         for quad in range(4):
             nc.sync.dma_start(
                 pool_scales[32 * quad : 32 * quad + 4, :].bitcast(I32),
                 keys_scales[0][4 * quad : 4 * quad + 4, :].bitcast(I32),
             )
-        nc.sync.dma_start(pool_words[:], keys_words[0].rearrange("p n t -> p (n t)").bitcast(I32))
-        nc.sync.dma_start(grows_raw[:], grows.rearrange("(p j) e -> p j e", j=PACK))
-        nc.sync.dma_start(sg_cols[:], sg.rearrange("o (p c) -> (o p) c", c=2))
-        nc.sync.dma_start(qs_sb[:], qs.rearrange("(p r) o -> p (r o)", r=PACK))
-        cross_rows = cross.rearrange("(p t) n -> p t n", t=PACK)
-        nc.sync.dma_start(cross_sb[0][:], cross_rows[:, 0, :])
         nc.sync.dma_start(cross_list[:], offs2)
+        nc.vector.memset(warm[:], 0.0)
+        nc.scalar.activation(warm[:], warm[:], ACT.Exp)
+        with tc.tile_pool(name="first", bufs=1) as first:
+            zeros = first.tile([P, P], F32, name="zeros")
+            nc.gpsimd.memset(zeros[:], 0.0)
+            nc.gpsimd.affine_select(
+                out=ident[:],
+                in_=zeros[:],
+                compare_op=ALU.not_equal,
+                fill=1.0,
+                base=0,
+                pattern=[[-1, P]],
+                channel_multiplier=1,
+            )
+
+        late = ctx.enter_context(tc.tile_pool(name="late", bufs=1))
+        query_raw = late.tile([P, PACK, Q], F32, name="query_raw")
+        grows_raw = late.tile([P, PACK, E], F32, name="grows_raw")
+        cross_sb = [late.tile([P, T], F32, name="cross%d" % t, tag="cross%d" % t) for t in range(PACK)]
+        old_sb = late.tile([P, PACK, I], F32, name="old_sb")
+        qs_sb = late.tile([P, PACK], F32, name="qs_sb")
+        share_sb = late.tile([P, PACK], F32, name="share_sb")
+        sg_cols = late.tile([P, 2], F32, name="sg_cols")
+        cross_rows = cross.rearrange("(p t) n -> p t n", t=PACK)
+        nc.sync.dma_start(query_raw[:], query.rearrange("(p j) q -> p j q", j=PACK))
+        nc.sync.dma_start(grows_raw[:], grows.rearrange("(p j) e -> p j e", j=PACK))
+        nc.sync.dma_start(qs_sb[:], qs.rearrange("(p r) o -> p (r o)", r=PACK))
+        nc.sync.dma_start(cross_sb[0][:], cross_rows[:, 0, :])
         nc.sync.dma_start(share_sb[:], share.rearrange("(p t) o -> p (t o)", t=PACK))
+        with nc.allow_non_contiguous_dma(reason="one gain to a partition, two columns"):
+            nc.sync.dma_start(sg_cols[:], sg.rearrange("o (c p) -> (o p) c", c=2))
         for t in range(1, PACK):
             nc.sync.dma_start(cross_sb[t][:], cross_rows[:, t, :])
         nc.sync.dma_start(old_sb[:], old.rearrange("(p t) i -> p t i", t=PACK))
-
-        make_identity(nc, ident[:])
-
-        sg_rows = ps.tile([P, 2, P], F32, name="sg_rows")
-        for c in range(2):
-            nc.tensor.transpose(sg_rows[:, c, :], sg_cols[:, c : c + 1].to_broadcast([P, P]), ident[:])
 
         def deal(copy, raw, half, name):
             dealt = sb.tile([P, 2, P, PACK], BF16, name=name, align_bytes=64)
@@ -92,15 +100,15 @@ def tile_attend_bvcrossed_d_pl_kernel(
         key_words = sb.tile([P, I], U32, name="key_words", align_bytes=64)
         key_scales = sb.tile([P, I], U8, name="key_scales", align_bytes=64)
 
+        nc.vector.tensor_copy(key_words[:], pool_words[:].bitcast(U32).indirect(key_list[:]))
+        nc.vector.tensor_copy(key_scales[:], pool_scales[:].indirect(key_list[:]))
         query_dealt = [
             deal(nc.vector.tensor_copy, query_raw, 0, "query_dealt0"),
             deal(nc.scalar.copy, query_raw, 1, "query_dealt1"),
         ]
-        nc.vector.tensor_copy(key_scales[:], pool_scales[:].indirect(key_list[:]))
         query_mx = [
             quantize(query_dealt[h][:].rearrange("p r s j -> p (r s j)"), "query%d" % h) for h in range(2)
         ]
-        nc.vector.tensor_copy(key_words[:], pool_words[:].bitcast(U32).indirect(key_list[:]))
 
         neg_max = sb.tile([P, PACK], F32, name="neg_max")
         row_sum = sb.tile([P, PACK], F32, name="row_sum")
@@ -110,7 +118,7 @@ def tile_attend_bvcrossed_d_pl_kernel(
         for r in range(PACK):
             codes, scales = query_mx[r // 2]
             cols = slice((r % 2) * P, (r % 2 + 1) * P)
-            scores = ps.tile([P, I], F32, name="scores%d" % r)
+            scores = ps.tile([P, I], F32, name="scores%d" % r, tag="product%d" % r)
             nc.tensor.matmul_mx(
                 out=scores[:],
                 lhsT=codes[:, cols].bitcast(FP8X4),
@@ -131,47 +139,62 @@ def tile_attend_bvcrossed_d_pl_kernel(
             )
         grows_dealt = [deal(nc.scalar.copy, grows_raw, h, "grows_dealt%d" % h) for h in range(2)]
 
-        w_woven = sb.tile([P, I, PACK], BF16, name="w_woven", align_bytes=64)
-        weave(nc.vector.tensor_copy, w_woven[:], w_rows[:])
-        w_codes, w_scales = quantize(w_woven[:].rearrange("p i t -> p (i t)"), "w")
+        w_woven = [sb.tile([P, P, PACK], BF16, name="w_woven%d" % c, align_bytes=64) for c in range(2)]
+        for c in range(2):
+            weave(nc.vector.tensor_copy, w_woven[c][:], w_rows[:, :, c * P : (c + 1) * P])
+        w_mx = [quantize(w_woven[c][:].rearrange("p i t -> p (i t)"), "w%d" % c) for c in range(2)]
 
-        y = sb.tile([P, PACK, I], F32, name="y")
+        y = [sb.tile([P, PACK, P], F32, name="y%d" % c) for c in range(2)]
         out_rows = out_0.rearrange("(p t) i -> p t i", t=PACK)
+        picked = [sb.tile([P, I], F32, name="picked%d" % t) for t in range(PACK)]
+        grows_mx = [
+            quantize(grows_dealt[h][:].rearrange("p r s j -> p (r s j)"), "grows%d" % h) for h in range(2)
+        ]
+        gained_turned = [sb.tile([P, 2, 2 * P], F32, name="gained_turned%d" % h) for h in range(2)]
         for h in range(2):
-            codes, scales = quantize(grows_dealt[h][:].rearrange("p r s j -> p (r s j)"), "grows%d" % h)
-            c0 = ps.tile([P, 2, I], F32, name="c0_%d" % h)
-            for u in range(2):
-                cols = slice(u * P, (u + 1) * P)
+            for c in range(2):
+                c0_turned = ps.tile([P, 2 * P], F32, name="c0_turned%d%d" % (h, c), tag="product%d" % (2 * h + c))
                 nc.tensor.matmul_mx(
-                    out=c0[:, u, :],
-                    lhsT=codes[:, cols].bitcast(FP8X4),
-                    lhsT_scale=scales[:, cols],
-                    rhs=w_codes[:].bitcast(FP8X4),
-                    rhs_scale=w_scales[:],
+                    out=c0_turned[:],
+                    lhsT=w_mx[c][0][:].bitcast(FP8X4),
+                    lhsT_scale=w_mx[c][1][:],
+                    rhs=grows_mx[h][0][:].bitcast(FP8X4),
+                    rhs_scale=grows_mx[h][1][:],
                     start=True,
                     stop=True,
                 )
+                nc.scalar.activation(gained_turned[h][:, c, :], c0_turned[:], ACT.Copy, scale=sg_cols[:, c : c + 1])
+        for t in range(PACK):
+            nc.vector.tensor_copy(picked[t][:], cross_sb[t][:].indirect(cross_list[:]))
+        prod = late.tile([P, PACK, I], F32, name="prod", tag="cross%d" % (PACK - 1))
+        for h in range(2):
+            gained = ps.tile([P, 2, I], F32, name="gained%d" % h)
+            for c in range(2):
+                for u in range(2):
+                    nc.tensor.transpose(
+                        gained[:, u, c * P : (c + 1) * P], gained_turned[h][:, c, u * P : (u + 1) * P], ident[:]
+                    )
             for u in range(2):
                 t = 2 * h + u
-                picked = sb.tile([P, I], F32, name="picked%d" % t)
-                factor = sb.tile([P, I], F32, name="factor%d" % t)
-                prod = sb.tile([P, I], F32, name="prod%d" % t)
-                nc.vector.tensor_copy(picked[:], cross_sb[t][:].indirect(cross_list[:]))
                 nc.vector.scalar_tensor_tensor(
-                    factor[:].rearrange("p (n c) -> p n c", c=2),
-                    picked[:].rearrange("p (n c) -> p n c", c=2),
-                    share_sb[:, t : t + 1],
-                    sg_rows[:].rearrange("p c n -> p n c"),
-                    ALU.add,
-                    ALU.mult,
+                    prod[:, t, :], picked[t][:], share_sb[:, t : t + 1], gained[:, u, :], ALU.add, ALU.mult
                 )
-                nc.vector.tensor_tensor(prod[:], c0[:, u, :], factor[:], ALU.mult)
-                nc.vector.tensor_tensor(y[:, t, :], prod[:], old_sb[:, t, :], ALU.add)
-                nc.sync.dma_start(out_rows[:, t, :], y[:, t, :])
 
-        y_woven = sb.tile([P, I, PACK], BF16, name="y_woven", align_bytes=64)
-        weave(nc.vector.tensor_copy, y_woven[:], y[:])
-        y_codes, y_scales = quantize(y_woven[:].rearrange("p i t -> p (i t)"), "y")
+        y_woven = [sb.tile([P, P, PACK], BF16, name="y_woven%d" % c, align_bytes=64) for c in range(2)]
+        y_codes = sb.tile([P, I], I32, name="y_codes", align_bytes=64)
+        y_scales = sb.tile([P, I], U8, name="y_scales", align_bytes=64)
+        for c, copy in enumerate((nc.scalar.copy, nc.vector.tensor_copy)):
+            cols = slice(c * P, (c + 1) * P)
+            nc.vector.tensor_tensor(y[c][:], prod[:, :, cols], old_sb[:, :, cols], ALU.add)
+            nc.sync.dma_start(out_rows[:, :, cols], y[c][:])
+            weave(copy, y_woven[c][:], y[c][:])
+        for c in range(2):
+            cols = slice(c * P, (c + 1) * P)
+            nc.vector.quantize_mx(
+                out=y_codes[:, cols].bitcast(FP8X4),
+                scales=y_scales[:, cols],
+                in_=y_woven[c][:].rearrange("p i t -> p (i t)"),
+            )
         nc.sync.dma_start(out_1[0].rearrange("p n t -> p (n t)").bitcast(I32), y_codes[:])
         for quad in range(4):
             nc.sync.dma_start(

@@ -38,8 +38,8 @@ def tile_attend_bvcrossed_d_pl_kernel(
 
         nc.vector.memset(pool_scales[:].bitcast(I32), 0)
 
-        nc.sync.dma_start(key_list[:], offs)
         nc.sync.dma_start(pool_words[:], keys_words[0].rearrange("p n t -> p (n t)").bitcast(I32))
+        nc.sync.dma_start(key_list[:], offs)
         for quad in range(4):
             nc.sync.dma_start(
                 pool_scales[32 * quad : 32 * quad + 4, :].bitcast(I32),
@@ -144,7 +144,7 @@ def tile_attend_bvcrossed_d_pl_kernel(
             weave(nc.vector.tensor_copy, w_woven[c][:], w_rows[:, :, c * P : (c + 1) * P])
         w_mx = [quantize(w_woven[c][:].rearrange("p i t -> p (i t)"), "w%d" % c) for c in range(2)]
 
-        y = [sb.tile([P, PACK, P], F32, name="y%d" % c) for c in range(2)]
+        y = sb.tile([P, PACK, I], F32, name="y")
         out_rows = out_0.rearrange("(p t) i -> p t i", t=PACK)
         picked = [sb.tile([P, I], F32, name="picked%d" % t) for t in range(PACK)]
         grows_mx = [
@@ -183,11 +183,14 @@ def tile_attend_bvcrossed_d_pl_kernel(
         y_woven = [sb.tile([P, P, PACK], BF16, name="y_woven%d" % c, align_bytes=64) for c in range(2)]
         y_codes = sb.tile([P, I], I32, name="y_codes", align_bytes=64)
         y_scales = sb.tile([P, I], U8, name="y_scales", align_bytes=64)
+        nc.gpsimd.tensor_tensor(y[:, 0, :], prod[:, 0, :], old_sb[:, 0, :], ALU.add)
+        nc.vector.tensor_tensor(y[:, 1, :], prod[:, 1, :], old_sb[:, 1, :], ALU.add)
+        nc.sync.dma_start(out_rows[:, 0:2, :], y[:, 0:2, :])
         for c, copy in enumerate((nc.scalar.copy, nc.vector.tensor_copy)):
             cols = slice(c * P, (c + 1) * P)
-            nc.vector.tensor_tensor(y[c][:], prod[:, :, cols], old_sb[:, :, cols], ALU.add)
-            nc.sync.dma_start(out_rows[:, :, cols], y[c][:])
-            weave(copy, y_woven[c][:], y[c][:])
+            nc.vector.tensor_tensor(y[:, 2:4, cols], prod[:, 2:4, cols], old_sb[:, 2:4, cols], ALU.add)
+            weave(copy, y_woven[c][:], y[:, :, cols])
+        nc.sync.dma_start(out_rows[:, 2:4, :], y[:, 2:4, :])
         for c in range(2):
             cols = slice(c * P, (c + 1) * P)
             nc.vector.quantize_mx(
@@ -197,7 +200,7 @@ def tile_attend_bvcrossed_d_pl_kernel(
             )
         nc.sync.dma_start(out_1[0].rearrange("p n t -> p (n t)").bitcast(I32), y_codes[:])
         for quad in range(4):
-            nc.sync.dma_start(
+            (nc.sync, nc.scalar)[quad % 2].dma_start(
                 out_2[0][4 * quad : 4 * quad + 4, :].bitcast(I32),
                 y_scales[32 * quad : 32 * quad + 4, :].bitcast(I32),
             )

from contextlib import ExitStack

import concourse.mybir as mybir

D, E, T, I, Q = 512, 512, 1024, 256, 512
FLOPS = 2 * D * Q * I + 2 * Q * E * I

F32 = mybir.dt.float32
BF16 = mybir.dt.bfloat16
I32 = mybir.dt.int32
U32 = mybir.dt.uint32
U16 = mybir.dt.uint16
U8 = mybir.dt.uint8
FP8X4 = mybir.dt.float8_e4m3fn_x4
ALU = mybir.AluOpType
ACT = mybir.ActivationFunctionType
AX = mybir.AxisListType

P = 128
PACK = 4
RUN = 4


def tile_attend_bvcrossed_d_pl_kernel(
    tc, query, qs, grows, keys_words, keys_scales, cross, share, sg, old, offs, offs2, out_0, out_1, out_2
):
    nc = tc.nc
    with ExitStack() as ctx:
        sb = ctx.enter_context(tc.tile_pool(name="sb", bufs=1))
        ps = ctx.enter_context(tc.psum_pool(name="ps", bufs=1))

        key_list = sb.tile([P, I // 16], U16, name="key_list")
        cross_list = sb.tile([P, I // 16], U16, name="cross_list")
        pool_words = sb.tile([P, T], I32, name="pool_words", align_bytes=64)
        warm = sb.tile([P, 1], F32, name="warm")
        pool_scales = sb.tile([P, T], U8, name="pool_scales", align_bytes=64)
        ident = sb.tile([P, P], F32, name="ident")

        nc.vector.memset(pool_scales[:].bitcast(I32), 0)

        nc.sync.dma_start(pool_words[:], keys_words[0].rearrange("p n t -> p (n t)").bitcast(I32))
        nc.sync.dma_start(key_list[:], offs)
        for quad in range(4):
            nc.sync.dma_start(
                pool_scales[32 * quad : 32 * quad + 4, :].bitcast(I32),
                keys_scales[0][4 * quad : 4 * quad + 4, :].bitcast(I32),
            )
        nc.sync.dma_start(cross_list[:], offs2)
        nc.vector.memset(warm[:], 0.0)
        nc.scalar.activation(warm[:], warm[:], ACT.Exp)
        with tc.tile_pool(name="first", bufs=1) as first:
            zeros = first.tile([P, P], F32, name="zeros")
            nc.gpsimd.memset(zeros[:], 0.0)
            nc.gpsimd.affine_select(
                out=ident[:],
                in_=zeros[:],
                compare_op=ALU.not_equal,
                fill=1.0,
                base=0,
                pattern=[[-1, P]],
                channel_multiplier=1,
            )

        late = ctx.enter_context(tc.tile_pool(name="late", bufs=1))
        query_raw = late.tile([P, PACK, Q], F32, name="query_raw")
        grows_raw = late.tile([P, PACK, E], F32, name="grows_raw")
        cross_sb = [late.tile([P, T], F32, name="cross%d" % t, tag="cross%d" % t) for t in range(PACK)]
        old_sb = late.tile([P, PACK, I], F32, name="old_sb")
        qs_sb = late.tile([P, PACK], F32, name="qs_sb")
        share_sb = late.tile([P, PACK], F32, name="share_sb")
        sg_cols = late.tile([P, 2], F32, name="sg_cols")
        cross_rows = cross.rearrange("(p t) n -> p t n", t=PACK)
        nc.sync.dma_start(query_raw[:], query.rearrange("(p j) q -> p j q", j=PACK))
        nc.sync.dma_start(grows_raw[:], grows.rearrange("(p j) e -> p j e", j=PACK))
        nc.sync.dma_start(qs_sb[:], qs.rearrange("(p r) o -> p (r o)", r=PACK))
        nc.sync.dma_start(cross_sb[0][:], cross_rows[:, 0, :])
        nc.sync.dma_start(share_sb[:], share.rearrange("(p t) o -> p (t o)", t=PACK))
        with nc.allow_non_contiguous_dma(reason="one gain to a partition, two columns"):
            nc.sync.dma_start(sg_cols[:], sg.rearrange("o (c p) -> (o p) c", c=2))
        for t in range(1, PACK):
            nc.sync.dma_start(cross_sb[t][:], cross_rows[:, t, :])
        nc.sync.dma_start(old_sb[:], old.rearrange("(p t) i -> p t i", t=PACK))

        def deal(copy, raw, half, name):
            dealt = sb.tile([P, 2, P, PACK], BF16, name=name, align_bytes=64)
            src = raw[:].rearrange("p j (s r) -> p s j r", r=PACK)[:, :, :, 2 * half : 2 * half + 2]
            copy(dealt[:].rearrange("p r s j -> p s j r"), src)
            return dealt

        def quantize(flat, name):
            width = flat.shape[1] // PACK
            codes = sb.tile([P, width], I32, name=name + "_codes", align_bytes=64)
            scales = sb.tile([P, width], U8, name=name + "_scales", align_bytes=64)
            nc.vector.quantize_mx(out=codes[:].bitcast(FP8X4), scales=scales[:], in_=flat)
            return codes, scales

        def weave(copy, dst, src):
            copy(dst.rearrange("p (c i) t -> p c t i", i=RUN), src.rearrange("p t (c i) -> p c t i", i=RUN))

        key_words = sb.tile([P, I], U32, name="key_words", align_bytes=64)
        key_scales = sb.tile([P, I], U8, name="key_scales", align_bytes=64)

        nc.vector.tensor_copy(key_words[:], pool_words[:].bitcast(U32).indirect(key_list[:]))
        nc.vector.tensor_copy(key_scales[:], pool_scales[:].indirect(key_list[:]))
        query_dealt = [
            deal(nc.vector.tensor_copy, query_raw, 0, "query_dealt0"),
            deal(nc.scalar.copy, query_raw, 1, "query_dealt1"),
        ]
        query_mx = [
            quantize(query_dealt[h][:].rearrange("p r s j -> p (r s j)"), "query%d" % h) for h in range(2)
        ]

        neg_max = sb.tile([P, PACK], F32, name="neg_max")
        row_sum = sb.tile([P, PACK], F32, name="row_sum")
        inv_sum = sb.tile([P, PACK], F32, name="inv_sum")
        probs = sb.tile([P, PACK, I], F32, name="probs")
        w_rows = sb.tile([P, PACK, I], BF16, name="w_rows")
        for r in range(PACK):
            codes, scales = query_mx[r // 2]
            cols = slice((r % 2) * P, (r % 2 + 1) * P)
            scores = ps.tile([P, I], F32, name="scores%d" % r, tag="product%d" % r)
            nc.tensor.matmul_mx(
                out=scores[:],
                lhsT=codes[:, cols].bitcast(FP8X4),
                lhsT_scale=scales[:, cols],
                rhs=key_words[:].bitcast(FP8X4),
                rhs_scale=key_scales[:],
                start=True,
                stop=True,
            )
            nc.vector.tensor_reduce(neg_max[:, r : r + 1], scores[:], AX.X, ALU.max, negate=True)
            nc.scalar.activation(
                probs[:, r, :], scores[:], ACT.Exp, bias=neg_max[:, r : r + 1], accum_out=row_sum[:, r : r + 1]
            )
        for r in range(PACK):
            nc.vector.reciprocal(inv_sum[:, r : r + 1], row_sum[:, r : r + 1])
            nc.vector.tensor_scalar(
                w_rows[:, r, :], probs[:, r, :], inv_sum[:, r : r + 1], qs_sb[:, r : r + 1], ALU.mult, ALU.mult
            )
        grows_dealt = [deal(nc.scalar.copy, grows_raw, h, "grows_dealt%d" % h) for h in range(2)]

        w_woven = [sb.tile([P, P, PACK], BF16, name="w_woven%d" % c, align_bytes=64) for c in range(2)]
        for c in range(2):
            weave(nc.vector.tensor_copy, w_woven[c][:], w_rows[:, :, c * P : (c + 1) * P])
        w_mx = [quantize(w_woven[c][:].rearrange("p i t -> p (i t)"), "w%d" % c) for c in range(2)]

        y = sb.tile([P, PACK, I], F32, name="y")
        out_rows = out_0.rearrange("(p t) i -> p t i", t=PACK)
        picked = [sb.tile([P, I], F32, name="picked%d" % t) for t in range(PACK)]
        grows_mx = [
            quantize(grows_dealt[h][:].rearrange("p r s j -> p (r s j)"), "grows%d" % h) for h in range(2)
        ]
        gained_turned = [sb.tile([P, 2, 2 * P], F32, name="gained_turned%d" % h) for h in range(2)]
        for h in range(2):
            for c in range(2):
                c0_turned = ps.tile([P, 2 * P], F32, name="c0_turned%d%d" % (h, c), tag="product%d" % (2 * h + c))
                nc.tensor.matmul_mx(
                    out=c0_turned[:],
                    lhsT=w_mx[c][0][:].bitcast(FP8X4),
                    lhsT_scale=w_mx[c][1][:],
                    rhs=grows_mx[h][0][:].bitcast(FP8X4),
                    rhs_scale=grows_mx[h][1][:],
                    start=True,
                    stop=True,
                )
                nc.scalar.activation(gained_turned[h][:, c, :], c0_turned[:], ACT.Copy, scale=sg_cols[:, c : c + 1])
        for t in range(PACK):
            nc.vector.tensor_copy(picked[t][:], cross_sb[t][:].indirect(cross_list[:]))
        prod = late.tile([P, PACK, I], F32, name="prod", tag="cross%d" % (PACK - 1))
        for h in range(2):
            gained = ps.tile([P, 2, I], F32, name="gained%d" % h)
            for c in range(2):
                for u in range(2):
                    nc.tensor.transpose(
                        gained[:, u, c * P : (c + 1) * P], gained_turned[h][:, c, u * P : (u + 1) * P], ident[:]
                    )
            for u in range(2):
                t = 2 * h + u
                nc.vector.scalar_tensor_tensor(
                    prod[:, t, :], picked[t][:], share_sb[:, t : t + 1], gained[:, u, :], ALU.add, ALU.mult
                )

        y_woven = [sb.tile([P, P, PACK], BF16, name="y_woven%d" % c, align_bytes=64) for c in range(2)]
        y_codes = sb.tile([P, I], I32, name="y_codes", align_bytes=64)
        y_scales = sb.tile([P, I], U8, name="y_scales", align_bytes=64)
        nc.gpsimd.tensor_tensor(y[:, 0, :], prod[:, 0, :], old_sb[:, 0, :], ALU.add)
        nc.vector.tensor_tensor(y[:, 1, :], prod[:, 1, :], old_sb[:, 1, :], ALU.add)
        nc.sync.dma_start(out_rows[:, 0:2, :], y[:, 0:2, :])
        for c, copy in enumerate((nc.scalar.copy, nc.vector.tensor_copy)):
            cols = slice(c * P, (c + 1) * P)
            nc.vector.tensor_tensor(y[:, 2:4, cols], prod[:, 2:4, cols], old_sb[:, 2:4, cols], ALU.add)
            weave(copy, y_woven[c][:], y[:, :, cols])
        nc.sync.dma_start(out_rows[:, 2:4, :], y[:, 2:4, :])
        for c in range(2):
            cols = slice(c * P, (c + 1) * P)
            nc.vector.quantize_mx(
                out=y_codes[:, cols].bitcast(FP8X4),
                scales=y_scales[:, cols],
                in_=y_woven[c][:].rearrange("p i t -> p (i t)"),
            )
        nc.sync.dma_start(out_1[0].rearrange("p n t -> p (n t)").bitcast(I32), y_codes[:])
        for quad in range(4):
            (nc.sync, nc.scalar)[quad % 2].dma_start(
                out_2[0][4 * quad : 4 * quad + 4, :].bitcast(I32),
                y_scales[32 * quad : 32 * quad + 4, :].bitcast(I32),
            )
